import numpy as np
import ml_dtypes


def mxq(x, axis, fmt="e4m3"):
    dtype, down = {"e4m3": (ml_dtypes.float8_e4m3fn, 7), "e5m2": (ml_dtypes.float8_e5m2, 14)}[fmt]
    v = np.moveaxis(np.asarray(x, np.float32).astype(ml_dtypes.bfloat16).astype(np.float64), axis, -1)
    blocks = v.reshape(v.shape[:-1] + (-1, 32))
    amax = np.abs(blocks).max(-1, keepdims=True)
    byte = np.maximum(np.where(amax > 0, np.frexp(amax)[1] - 1 + 127, 0) - down, 1)
    scale = np.exp2(byte - 127.0)
    codes = (blocks / scale).astype(np.float32).astype(dtype).astype(np.float64)
    return np.moveaxis((codes * scale).reshape(v.shape), -1, axis)


WIDE = False


def mx_kscale(k):
    if not WIDE:
        return np.ones(k)
    levels = np.array([10, -10, 5, -5, 0])
    if k % 512:
        return np.exp2(np.random.permutation(np.resize(levels, k // 32))).repeat(32)
    a = np.empty((k // 512, 16))
    for p in range(k // 512):
        a[p, :8] = np.random.permutation(np.resize(levels, 8))
        for g in range(8):
            far = levels[np.abs(levels - a[p, g]) >= 10]
            a[p, g + 8] = far[np.random.randint(len(far))]
    return np.exp2(a.ravel()).repeat(32)


def f64(x):
    return np.asarray(x).astype(np.float64)


def striped(idx):
    return np.tile(idx.reshape(-1, 16).T, (8, 1)).astype(np.uint16)


def unstriped(offs):
    return offs[:16].T.reshape(-1).astype(np.int64)


def striped8(idx):
    return np.concatenate([x.reshape(-1, 16).T for x in idx]).astype(np.uint16)


def runs(offs, k):
    lists = np.stack([offs[16 * r : 16 * r + 16].T.reshape(-1) for r in range(8)]).astype(np.int64)
    return lists[np.arange(k) % 512 // 64]


def pack_weight(w):
    k, n = w.shape
    w = f64(np.asarray(w, np.float32).astype(ml_dtypes.bfloat16)).reshape(k // 32, 32, n)
    amax = np.abs(w).max(1)
    byte = np.clip(np.where(amax > 0, np.frexp(amax)[1] - 1 + 127 - 7, 1), 1, 254)
    scaled = (w * np.exp2(127.0 - byte)[:, None, :]).reshape(k, n).astype(np.float32)
    words = np.ascontiguousarray(scaled.reshape(k // 512, 128, 4, n).transpose(0, 1, 3, 2)).astype(ml_dtypes.float8_e4m3fn).view(np.uint8)
    return words, np.ascontiguousarray(byte.astype(np.uint8).reshape(k // 512, 16, n))


def unpack_weight(words, scales):
    g, p, n, _ = words.shape
    vals = np.ascontiguousarray(words).view(ml_dtypes.float8_e4m3fn).astype(np.float64) * np.repeat(np.exp2(scales.astype(np.float64) - 127.0), 8, axis=1)[..., None]
    return vals.transpose(0, 1, 3, 2).reshape(g * 512, n)


def relu(v):
    return np.maximum(v, 0.0)

def planes(y):
    n, m = y.shape
    v = y.astype(np.float32).astype(ml_dtypes.bfloat16).astype(np.float64).reshape(n // 32, 32, m)
    top = np.abs(v).max(1)
    byte = np.clip(np.where(top > 0, np.frexp(top)[1] - 1 + 127 - 7, 1), 1, 254)
    codes = (v * np.exp2(127.0 - byte)[:, None, :]).reshape(n, m).astype(np.float32).astype(ml_dtypes.float8_e4m3fn).view(np.uint8)
    words = codes.reshape(n // 512, 128, 4, m).transpose(0, 1, 3, 2)
    return np.ascontiguousarray(words), np.ascontiguousarray(byte.astype(np.uint8).reshape(n // 512, 16, m))


K, T, S, H, C = 512, 2048, 512, 512, 512


def setup_inputs():
    n = np.random.standard_normal
    s = mx_kscale(K)[:, None]
    packed_xT = pack_weight(n((K, T)) * s)
    packed_w1 = pack_weight(n((K, H)) / np.sqrt(K) / s)
    return {
        "x_words": packed_xT[0],
        "x_scales": packed_xT[1],
        "w1_words": packed_w1[0],
        "w1_scales": packed_w1[1],
        "gs": (np.random.uniform(0.5, 1.5, (K, 1)) / s).astype(np.float32),
        "offs": striped(np.random.permutation(T)[:S]),
        "cand": striped(np.random.permutation(T)[:C]),
        "n1": striped8(np.stack([np.random.permutation(S) for _ in range(8)])),
        "n2": striped8(np.stack([np.random.permutation(S) for _ in range(8)])),
    }


def reference(x_words, x_scales, w1_words, w1_scales, gs, offs, cand, n1, n2):
    x_cand = unpack_weight(x_words, x_scales)[:, unstriped(cand)]
    xq = unpack_weight(x_words, x_scales)[:, unstriped(offs)]
    h = relu(unpack_weight(w1_words, w1_scales).T @ xq)
    z = f64(gs) * h
    s = 0.0625 * ((x_cand.T @ mxq(z, 0, "e4m3")))
    a = s[np.arange(C)[:, None], runs(n1, C)]
    b = s[np.arange(C)[:, None], runs(n2, C)]
    out_0 = s - (np.maximum(np.minimum(s, a), np.minimum(np.maximum(s, a), b)))
    return (out_0,) + planes(out_0)

@@ -1,0 +1,203 @@
+from contextlib import ExitStack
+
+import concourse.mybir as mybir
+
+K, T, S, H, C = 512, 2048, 512, 512, 512
+FLOPS = 2 * K * H * S + 2 * K * C * S
+BYTES = K * (S + C) * 33 // 32 + K * H * 33 // 32 + 4 * K + 4 * 128 * 32 * 2 + C * S * 4 + C * S * 33 // 32
+
+F32 = mybir.dt.float32
+BF16 = mybir.dt.bfloat16
+I32 = mybir.dt.int32
+U32 = mybir.dt.uint32
+U16 = mybir.dt.uint16
+U8 = mybir.dt.uint8
+FP8X4 = mybir.dt.float8_e4m3fn_x4
+ALU = mybir.AluOpType
+COPY = mybir.ActivationFunctionType.Copy
+
+P = 128
+PACK = 4
+CH = 128
+NCH = S // CH
+SCORE = 0.0625
+
+
+def tile_picked_candmed_none_po_kernel(
+    tc, x_words, x_scales, w1_words, w1_scales, gs, offs, cand, n1, n2, out_0, out_1, out_2
+):
+    nc = tc.nc
+    with ExitStack() as ctx:
+        lists = ctx.enter_context(tc.tile_pool(name="lists", bufs=1))
+        sb = ctx.enter_context(tc.tile_pool(name="sb", bufs=1))
+        ps = ctx.enter_context(tc.psum_pool(name="ps", bufs=1))
+
+        offs_t = lists.tile([P, S // 16], U16, name="offs_t")
+        cand_t = lists.tile([P, C // 16], U16, name="cand_t")
+        n1_t = lists.tile([P, S // 16], U16, name="n1_t")
+        n2_t = lists.tile([P, S // 16], U16, name="n2_t")
+
+        xw = sb.tile([P, T], I32, name="xw", align_bytes=64)
+        xs = sb.tile([P, T], U8, name="xs", align_bytes=64)
+        w1w = sb.tile([P, H], I32, name="w1w", align_bytes=64)
+        w1s = sb.tile([P, H], U8, name="w1s", align_bytes=64)
+        gs_t = sb.tile([P, PACK], F32, name="gs_t")
+        zero = sb.tile([P, 1], F32, name="zero")
+
+        nc.vector.memset(xs[:].bitcast(I32), 0)
+        nc.gpsimd.memset(w1s[:].bitcast(I32), 0)
+        nc.vector.memset(zero[:], 0.0)
+
+        nc.sync.dma_start(offs_t[:], offs)
+        nc.sync.dma_start(cand_t[:], cand)
+        nc.sync.dma_start(xw[:], x_words[0].rearrange("p n t -> p (n t)").bitcast(I32))
+        nc.sync.dma_start(w1w[:], w1_words[0].rearrange("p n t -> p (n t)").bitcast(I32))
+        for q in range(4):
+            nc.scalar.dma_start(xs[32 * q : 32 * q + 4, :].bitcast(I32), x_scales[0, 4 * q : 4 * q + 4, :].bitcast(I32))
+        for q in range(4):
+            nc.gpsimd.dma_start(w1s[32 * q : 32 * q + 4, :].bitcast(I32), w1_scales[0, 4 * q : 4 * q + 4, :].bitcast(I32))
+        nc.sync.dma_start(gs_t[:], gs.rearrange("(p t) o -> p (t o)", t=PACK))
+        nc.sync.dma_start(n1_t[:], n1)
+        nc.sync.dma_start(n2_t[:], n2)
+
+        win = [sb.tile([P, 2 * S if t < 3 else S], F32, name="win%d" % t) for t in range(PACK)]
+        s2 = sb.tile([P, S], F32, name="s2")
+        s3 = sb.tile([P, S], F32, name="s3")
+        pos = [win[1][:, S:], win[2][:, S:], s2[:], s3[:]]
+        nc.scalar.activation(win[0][:, S:], zero[:].to_broadcast([P, S]), COPY)
+
+        xq_w = sb.tile([P, S], I32, name="xq_w", align_bytes=64)
+        xq_s = sb.tile([P, S], U8, name="xq_s", align_bytes=64)
+        xc_w = sb.tile([P, C], I32, name="xc_w", align_bytes=64)
+        xc_raw = sb.tile([P, C], U8, name="xc_raw", align_bytes=64)
+        xc_s = sb.tile([P, C], U8, name="xc_s", align_bytes=64)
+        wd_w = sb.tile([P, H], I32, name="wd_w", align_bytes=64)
+        wd_s = sb.tile([P, H], U8, name="wd_s", align_bytes=64)
+
+        def deal(dst, src):
+            nc.vector.tensor_copy(dst.rearrange("p (t m) -> p m t", t=PACK), src.rearrange("p (m t) -> p m t", t=PACK))
+
+        nc.vector.tensor_copy(xq_s[:], xs[:].indirect(offs_t[:]))
+        nc.vector.tensor_copy(xc_raw[:], xs[:].indirect(cand_t[:]))
+        deal(xc_s[:], xc_raw[:])
+        deal(wd_w[:], w1w[:])
+        deal(wd_s[:], w1s[:])
+        for half in range(2):
+            nc.vector.tensor_copy(
+                xq_w[:, 256 * half : 256 * (half + 1)].bitcast(U32),
+                xw[:].bitcast(U32).indirect(offs_t[:, 16 * half : 16 * (half + 1)]),
+            )
+
+        hb = [ps.tile([P, PACK, CH], F32, name="hb%d" % c, tag="bank%d" % c) for c in range(NCH)]
+        for c in range(NCH):
+            cols = slice(c * CH, (c + 1) * CH)
+            for t in range(PACK):
+                m = slice(t * P, (t + 1) * P)
+                nc.tensor.matmul_mx(
+                    hb[c][:, t, :], lhsT=wd_w[:, m].bitcast(FP8X4), lhsT_scale=wd_s[:, m],
+                    rhs=xq_w[:, cols].bitcast(FP8X4), rhs_scale=xq_s[:, cols], start=True, stop=True,
+                )
+
+        nc.vector.tensor_copy(
+            xc_w[:].bitcast(U32).rearrange("p (t m) -> p m t", t=PACK), xw[:].bitcast(U32).indirect(cand_t[:])
+        )
+
+        zb = [sb.tile([P, CH, PACK], BF16, name="zb%d" % c, align_bytes=64) for c in range(NCH)]
+        z_w = sb.tile([P, S], I32, name="z_w", align_bytes=64)
+        z_s = sb.tile([P, S], U8, name="z_s", align_bytes=64)
+
+        def gate(c):
+            nc.vector.scalar_tensor_tensor(
+                zb[c][:], hb[c][:].rearrange("p t n -> p n t"), 0.0,
+                gs_t[:].unsqueeze(1).to_broadcast([P, CH, PACK]), ALU.max, ALU.mult,
+            )
+
+        def score(bank, t, cols):
+            m = slice(t * P, (t + 1) * P)
+            nc.tensor.matmul_mx(
+                bank, lhsT=xc_w[:, m].bitcast(FP8X4), lhsT_scale=xc_s[:, m],
+                rhs=z_w[:, cols].bitcast(FP8X4), rhs_scale=z_s[:, cols], start=True, stop=True,
+            )
+            nc.scalar.activation(win[t][:, cols], bank, COPY, scale=-SCORE)
+            nc.scalar.activation(pos[t][:, cols], bank, COPY, scale=SCORE)
+
+        def quant_z(c):
+            cols = slice(c * CH, (c + 1) * CH)
+            nc.vector.quantize_mx(z_w[:, cols].bitcast(FP8X4), z_s[:, cols], zb[c][:].rearrange("p n t -> p (n t)"))
+            bank = ps.tile([P, CH], F32, name="s0b%d" % c, tag="bank%d" % c)
+            score(bank[:], 0, cols)
+
+        gate(0)
+        for c in range(1, NCH):
+            gate(c)
+            quant_z(c - 1)
+        quant_z(NCH - 1)
+        for t in range(1, PACK):
+            bank = ps.tile([P, S], F32, name="sb%d" % t, tag="bank%d" % (NCH + t))
+            score(bank[:], t, slice(0, S))
+
+        u = [sb.tile([P, S], F32, name="u%d" % t) for t in range(PACK)]
+        v = [sb.tile([P, S], F32, name="v%d" % t) for t in range(PACK)]
+        low = [sb.tile([P, S], F32, name="low%d" % t) for t in range(PACK)]
+        y = sb.tile([P, NCH, PACK, CH], F32, name="y", align_bytes=64)
+        yb = [sb.tile([P, CH, PACK], BF16, name="yb%d" % c, align_bytes=64) for c in range(NCH)]
+        y_w = sb.tile([P, S], I32, name="y_w", align_bytes=64)
+        y_s = sb.tile([P, S], U8, name="y_s", align_bytes=64)
+        out_rows = out_0.rearrange("(p t) (c n) -> p t c n", t=PACK, n=CH)
+        out_words = out_1[0].rearrange("p n t -> p (n t)").bitcast(I32)
+
+        def diff(dst, lst, t, c0, c1):
+            cols = slice(c0 * CH, c1 * CH)
+            nc.vector.tensor_tensor(
+                dst[t][:, cols], win[t][:].indirect(lst[:, c0 * CH // 16 : c1 * CH // 16]), pos[t][:, cols], ALU.add
+            )
+
+        def upper(t, c0, c1):
+            cols = slice(c0 * CH, c1 * CH)
+            nc.vector.scalar_tensor_tensor(low[t][:, cols], u[t][:, cols], 0.0, v[t][:, cols], ALU.max, ALU.min)
+
+        def lower(t, c0, c1):
+            cols = slice(c0 * CH, c1 * CH)
+            nc.vector.scalar_tensor_tensor(
+                y[:, c0:c1, t, :], u[t][:, cols].rearrange("p (c n) -> p c n", n=CH), 0.0,
+                low[t][:, cols].rearrange("p (c n) -> p c n", n=CH), ALU.min, ALU.max,
+            )
+            nc.sync.dma_start(out_rows[:, t, c0:c1, :], y[:, c0:c1, t, :])
+
+        def weave(eng, c):
+            dst = yb[c][:].rearrange("p (a i) t -> p a t i", i=4)
+            src = y[:, c, :, :].rearrange("p t (a i) -> p a t i", i=4)
+            if eng == "scalar":
+                nc.scalar.copy(dst, src)
+            else:
+                nc.vector.tensor_copy(dst, src)
+
+        def quant_y(c):
+            cols = slice(c * CH, (c + 1) * CH)
+            nc.vector.quantize_mx(y_w[:, cols].bitcast(FP8X4), y_s[:, cols], yb[c][:].rearrange("p n t -> p (n t)"))
+
+        jobs = [(0, 0, 4), (1, 0, 4), (2, 0, 4), (3, 0, 2), (3, 2, 3), (3, 3, 4)]
+        diff(u, n1_t, 0, 0, 2)
+        diff(u, n1_t, 0, 2, 4)
+        diff(v, n2_t, 0, 0, 4)
+        for i, job in enumerate(jobs):
+            nxt = jobs[i + 1] if i + 1 < len(jobs) else None
+            if nxt:
+                diff(u, n1_t, *nxt)
+            upper(*job)
+            if nxt:
+                diff(v, n2_t, *nxt)
+            else:
+                quant_y(0)
+                quant_y(1)
+                nc.scalar.dma_start(out_words[:, 0 : 2 * CH], y_w[:, 0 : 2 * CH])
+            lower(*job)
+            if job[0] == 3:
+                for c in range(job[1], job[2]):
+                    weave("scalar" if c < NCH - 1 else "vector", c)
+        quant_y(2)
+        quant_y(3)
+        nc.sync.dma_start(out_words[:, 2 * CH :], y_w[:, 2 * CH :])
+        for q in range(4):
+            eng = nc.sync if q < 1 else nc.scalar
+            eng.dma_start(out_2[0, 4 * q : 4 * q + 4, :].bitcast(I32), y_s[32 * q : 32 * q + 4, :].bitcast(I32))

@@ -45,18 +45,18 @@ def tile_picked_candmed_none_po_kernel(
         zero = sb.tile([P, 1], F32, name="zero")
 
         nc.vector.memset(xs[:].bitcast(I32), 0)
-        nc.gpsimd.memset(w1s[:].bitcast(I32), 0)
+        nc.vector.memset(w1s[:].bitcast(I32), 0)
         nc.vector.memset(zero[:], 0.0)
 
         nc.sync.dma_start(offs_t[:], offs)
         nc.sync.dma_start(cand_t[:], cand)
+        nc.sync.dma_start(gs_t[:], gs.rearrange("(p t) o -> p (t o)", t=PACK))
+        for q in range(4):
+            nc.sync.dma_start(xs[32 * q : 32 * q + 4, :].bitcast(I32), x_scales[0, 4 * q : 4 * q + 4, :].bitcast(I32))
         nc.sync.dma_start(xw[:], x_words[0].rearrange("p n t -> p (n t)").bitcast(I32))
         nc.sync.dma_start(w1w[:], w1_words[0].rearrange("p n t -> p (n t)").bitcast(I32))
         for q in range(4):
-            nc.scalar.dma_start(xs[32 * q : 32 * q + 4, :].bitcast(I32), x_scales[0, 4 * q : 4 * q + 4, :].bitcast(I32))
-        for q in range(4):
-            nc.gpsimd.dma_start(w1s[32 * q : 32 * q + 4, :].bitcast(I32), w1_scales[0, 4 * q : 4 * q + 4, :].bitcast(I32))
-        nc.sync.dma_start(gs_t[:], gs.rearrange("(p t) o -> p (t o)", t=PACK))
+            nc.sync.dma_start(w1s[32 * q : 32 * q + 4, :].bitcast(I32), w1_scales[0, 4 * q : 4 * q + 4, :].bitcast(I32))
         nc.sync.dma_start(n1_t[:], n1)
         nc.sync.dma_start(n2_t[:], n2)
 
@@ -189,9 +189,10 @@ def tile_picked_candmed_none_po_kernel(
                 diff(v, n2_t, *nxt)
             else:
                 quant_y(0)
+            lower(*job)
+            if not nxt:
                 quant_y(1)
                 nc.scalar.dma_start(out_words[:, 0 : 2 * CH], y_w[:, 0 : 2 * CH])
-            lower(*job)
             if job[0] == 3:
                 for c in range(job[1], job[2]):
                     weave("scalar" if c < NCH - 1 else "vector", c)

@@ -1,6 +1,7 @@
 from contextlib import ExitStack
 
 import concourse.mybir as mybir
+from concourse.masks import make_identity
 
 K, T, S, H, C = 512, 2048, 512, 512, 512
 FLOPS = 2 * K * H * S + 2 * K * C * S
@@ -15,12 +16,14 @@ U8 = mybir.dt.uint8
 FP8X4 = mybir.dt.float8_e4m3fn_x4
 ALU = mybir.AluOpType
 COPY = mybir.ActivationFunctionType.Copy
+RELU = mybir.ActivationFunctionType.Relu
 
 P = 128
 PACK = 4
 CH = 128
 NCH = S // CH
 SCORE = 0.0625
+XS_SPLIT = 1344
 
 
 def tile_picked_candmed_none_po_kernel(
@@ -30,6 +33,7 @@ def tile_picked_candmed_none_po_kernel(
     with ExitStack() as ctx:
         lists = ctx.enter_context(tc.tile_pool(name="lists", bufs=1))
         sb = ctx.enter_context(tc.tile_pool(name="sb", bufs=1))
+        reuse = ctx.enter_context(tc.tile_pool(name="reuse", bufs=1))
         ps = ctx.enter_context(tc.psum_pool(name="ps", bufs=1))
 
         offs_t = lists.tile([P, S // 16], U16, name="offs_t")
@@ -40,25 +44,29 @@ def tile_picked_candmed_none_po_kernel(
         xw = sb.tile([P, T], I32, name="xw", align_bytes=64)
         xs = sb.tile([P, T], U8, name="xs", align_bytes=64)
         w1w = sb.tile([P, H], I32, name="w1w", align_bytes=64)
-        w1s = sb.tile([P, H], U8, name="w1s", align_bytes=64)
+        w1s = reuse.tile([P, H], U8, name="w1s", offset=768, align_bytes=64)
         gs_t = sb.tile([P, PACK], F32, name="gs_t")
         zero = sb.tile([P, 1], F32, name="zero")
 
-        nc.vector.memset(xs[:].bitcast(I32), 0)
+        nc.vector.memset(xs[:, : XS_SPLIT].bitcast(I32), 0)
+        nc.gpsimd.memset(xs[:, XS_SPLIT :].bitcast(I32), 0)
         nc.vector.memset(w1s[:].bitcast(I32), 0)
         nc.vector.memset(zero[:], 0.0)
 
+        nc.sync.dma_start(w1w[:], w1_words[0].rearrange("p n t -> p (n t)").bitcast(I32))
         nc.sync.dma_start(offs_t[:], offs)
-        nc.sync.dma_start(cand_t[:], cand)
-        nc.sync.dma_start(gs_t[:], gs.rearrange("(p t) o -> p (t o)", t=PACK))
         for q in range(4):
             nc.sync.dma_start(xs[32 * q : 32 * q + 4, :].bitcast(I32), x_scales[0, 4 * q : 4 * q + 4, :].bitcast(I32))
+        nc.sync.dma_start(cand_t[:], cand)
         nc.sync.dma_start(xw[:], x_words[0].rearrange("p n t -> p (n t)").bitcast(I32))
-        nc.sync.dma_start(w1w[:], w1_words[0].rearrange("p n t -> p (n t)").bitcast(I32))
         for q in range(4):
             nc.sync.dma_start(w1s[32 * q : 32 * q + 4, :].bitcast(I32), w1_scales[0, 4 * q : 4 * q + 4, :].bitcast(I32))
+        nc.sync.dma_start(gs_t[:], gs.rearrange("(p t) o -> p (t o)", t=PACK))
         nc.sync.dma_start(n1_t[:], n1)
         nc.sync.dma_start(n2_t[:], n2)
+
+        ident = sb.tile([P, P], F32, name="ident")
+        make_identity(nc, ident[:])
 
         win = [sb.tile([P, 2 * S if t < 3 else S], F32, name="win%d" % t) for t in range(PACK)]
         s2 = sb.tile([P, S], F32, name="s2")
@@ -66,81 +74,114 @@ def tile_picked_candmed_none_po_kernel(
         pos = [win[1][:, S:], win[2][:, S:], s2[:], s3[:]]
         nc.scalar.activation(win[0][:, S:], zero[:].to_broadcast([P, S]), COPY)
 
-        xq_w = sb.tile([P, S], I32, name="xq_w", align_bytes=64)
+        xq_w = [
+            reuse.tile([P, S // 2], I32, name="xq_w0", offset=0, align_bytes=64),
+            sb.tile([P, S // 2], I32, name="xq_w1", align_bytes=64),
+        ]
         xq_s = sb.tile([P, S], U8, name="xq_s", align_bytes=64)
-        xc_w = sb.tile([P, C], I32, name="xc_w", align_bytes=64)
         xc_raw = sb.tile([P, C], U8, name="xc_raw", align_bytes=64)
-        xc_s = sb.tile([P, C], U8, name="xc_s", align_bytes=64)
+        xc_s0 = sb.tile([P, P], U8, name="xc_s0", align_bytes=64)
         wd_w = sb.tile([P, H], I32, name="wd_w", align_bytes=64)
         wd_s = sb.tile([P, H], U8, name="wd_s", align_bytes=64)
 
         def deal(dst, src):
             nc.vector.tensor_copy(dst.rearrange("p (t m) -> p m t", t=PACK), src.rearrange("p (m t) -> p m t", t=PACK))
 
+        deal(wd_w[:], w1w[:])
         nc.vector.tensor_copy(xq_s[:], xs[:].indirect(offs_t[:]))
         nc.vector.tensor_copy(xc_raw[:], xs[:].indirect(cand_t[:]))
-        deal(xc_s[:], xc_raw[:])
-        deal(wd_w[:], w1w[:])
+        xc_mt = xc_raw[:].rearrange("p (m t) -> p m t", t=PACK)
+        nc.vector.tensor_copy(xc_s0[:], xc_mt[:, :, 0])
         deal(wd_s[:], w1s[:])
-        for half in range(2):
+        for half in (1, 0):
             nc.vector.tensor_copy(
-                xq_w[:, 256 * half : 256 * (half + 1)].bitcast(U32),
+                xq_w[half][:].bitcast(U32),
                 xw[:].bitcast(U32).indirect(offs_t[:, 16 * half : 16 * (half + 1)]),
             )
 
         hb = [ps.tile([P, PACK, CH], F32, name="hb%d" % c, tag="bank%d" % c) for c in range(NCH)]
-        for c in range(NCH):
+        for c in (2, 0, 1, 3):
             cols = slice(c * CH, (c + 1) * CH)
             for t in range(PACK):
                 m = slice(t * P, (t + 1) * P)
                 nc.tensor.matmul_mx(
                     hb[c][:, t, :], lhsT=wd_w[:, m].bitcast(FP8X4), lhsT_scale=wd_s[:, m],
-                    rhs=xq_w[:, cols].bitcast(FP8X4), rhs_scale=xq_s[:, cols], start=True, stop=True,
+                    rhs=xq_w[c // 2][:, c % 2 * CH : (c % 2 + 1) * CH].bitcast(FP8X4), rhs_scale=xq_s[:, cols], start=True, stop=True,
                 )
 
+        xc_w = reuse.tile([P, C], I32, name="xc_w", offset=1024, align_bytes=64)
         nc.vector.tensor_copy(
             xc_w[:].bitcast(U32).rearrange("p (t m) -> p m t", t=PACK), xw[:].bitcast(U32).indirect(cand_t[:])
         )
 
-        zb = [sb.tile([P, CH, PACK], BF16, name="zb%d" % c, align_bytes=64) for c in range(NCH)]
+        zb = [sb.tile([P, 2 * CH, PACK], BF16, name="zb%d" % h, tag="zb%d" % h, align_bytes=64) for h in range(2)]
+
+        def z_chunk(c):
+            return zb[c // 2][:, c % 2 * CH : (c % 2 + 1) * CH, :]
+
         z_w = sb.tile([P, S], I32, name="z_w", align_bytes=64)
         z_s = sb.tile([P, S], U8, name="z_s", align_bytes=64)
 
+        def woven(tile3):
+            return tile3.rearrange("p (a i) t -> p a t i", i=4)
+
+        def planes(tile3):
+            return tile3.rearrange("p t (a i) -> p a t i", i=4)
+
+        h0 = sb.tile([P, PACK, CH], F32, name="h0")
+        z0 = sb.tile([P, PACK, CH], BF16, name="z0")
+        nc.scalar.activation(h0[:], hb[2][:], RELU)
+        for t in range(PACK):
+            nc.scalar.activation(z0[:, t, :], h0[:, t, :], COPY, scale=gs_t[:, t : t + 1])
+        nc.scalar.copy(woven(z_chunk(2)), planes(z0[:]))
+
         def gate(c):
             nc.vector.scalar_tensor_tensor(
-                zb[c][:], hb[c][:].rearrange("p t n -> p n t"), 0.0,
+                z_chunk(c), hb[c][:].rearrange("p t n -> p n t"), 0.0,
                 gs_t[:].unsqueeze(1).to_broadcast([P, CH, PACK]), ALU.max, ALU.mult,
             )
 
-        def score(bank, t, cols):
-            m = slice(t * P, (t + 1) * P)
+        def score(bank, t, scales, cols):
             nc.tensor.matmul_mx(
-                bank, lhsT=xc_w[:, m].bitcast(FP8X4), lhsT_scale=xc_s[:, m],
+                bank, lhsT=xc_w[:, t * P : (t + 1) * P].bitcast(FP8X4), lhsT_scale=scales,
                 rhs=z_w[:, cols].bitcast(FP8X4), rhs_scale=z_s[:, cols], start=True, stop=True,
             )
+
+        def drain_neg(bank, t, cols):
             nc.scalar.activation(win[t][:, cols], bank, COPY, scale=-SCORE)
+
+        def drain_pos(bank, t, cols):
             nc.scalar.activation(pos[t][:, cols], bank, COPY, scale=SCORE)
 
-        def quant_z(c):
-            cols = slice(c * CH, (c + 1) * CH)
-            nc.vector.quantize_mx(z_w[:, cols].bitcast(FP8X4), z_s[:, cols], zb[c][:].rearrange("p n t -> p (n t)"))
-            bank = ps.tile([P, CH], F32, name="s0b%d" % c, tag="bank%d" % c)
-            score(bank[:], 0, cols)
-
+        halves = [slice(0, 2 * CH), slice(2 * CH, S)]
         gate(0)
-        for c in range(1, NCH):
-            gate(c)
-            quant_z(c - 1)
-        quant_z(NCH - 1)
+        gate(1)
+        gate(3)
+        first = []
+        for h, cols in enumerate(halves):
+            nc.vector.quantize_mx(z_w[:, cols].bitcast(FP8X4), z_s[:, cols], zb[h][:].rearrange("p n t -> p (n t)"))
+            bank = ps.tile([P, 2 * CH], F32, name="first%d" % h, tag="bank%d" % (4 - h))
+            score(bank[:], 0, xc_s0[:], cols)
+            drain_neg(bank[:], 0, cols)
+            first.append(bank)
+        drain_pos(first[1][:], 0, halves[1])
+        xc_s = sb.tile([P, (PACK - 1) * P], U8, name="xc_s", tag="zb1", align_bytes=64)
+        nc.vector.tensor_copy(xc_s[:].rearrange("p (t m) -> p m t", t=PACK - 1), xc_mt[:, :, 1:])
+        nc.vector.tensor_scalar_mul(pos[0][:, halves[0]], first[0][:], SCORE)
+        score_ps = {}
         for t in range(1, PACK):
-            bank = ps.tile([P, S], F32, name="sb%d" % t, tag="bank%d" % (NCH + t))
-            score(bank[:], t, slice(0, S))
+            score_ps[t] = ps.tile([P, S], F32, name="sb%d" % t, tag="bank%d" % (NCH + t))
+            score(score_ps[t][:], t, xc_s[:, (t - 1) * P : t * P], slice(0, S))
 
-        u = [sb.tile([P, S], F32, name="u%d" % t) for t in range(PACK)]
-        v = [sb.tile([P, S], F32, name="v%d" % t) for t in range(PACK)]
-        low = [sb.tile([P, S], F32, name="low%d" % t) for t in range(PACK)]
+        def drain(t):
+            drain_neg(score_ps[t][:], t, slice(0, S))
+            drain_pos(score_ps[t][:], t, slice(0, S))
+
+        drain(1)
+
+        u, v, low = {}, {}, {}
         y = sb.tile([P, NCH, PACK, CH], F32, name="y", align_bytes=64)
-        yb = [sb.tile([P, CH, PACK], BF16, name="yb%d" % c, align_bytes=64) for c in range(NCH)]
+        yb = sb.tile([P, S, PACK], BF16, name="yb", align_bytes=64)
         y_w = sb.tile([P, S], I32, name="y_w", align_bytes=64)
         y_s = sb.tile([P, S], U8, name="y_s", align_bytes=64)
         out_rows = out_0.rearrange("(p t) (c n) -> p t c n", t=PACK, n=CH)
@@ -148,56 +189,122 @@ def tile_picked_candmed_none_po_kernel(
 
         def diff(dst, lst, t, c0, c1):
             cols = slice(c0 * CH, c1 * CH)
-            nc.vector.tensor_tensor(
-                dst[t][:, cols], win[t][:].indirect(lst[:, c0 * CH // 16 : c1 * CH // 16]), pos[t][:, cols], ALU.add
-            )
+            nc.vector.tensor_tensor(dst, win[t][:].indirect(lst[:, c0 * CH // 16 : c1 * CH // 16]), pos[t][:, cols], ALU.add)
 
-        def upper(t, c0, c1):
-            cols = slice(c0 * CH, c1 * CH)
-            nc.vector.scalar_tensor_tensor(low[t][:, cols], u[t][:, cols], 0.0, v[t][:, cols], ALU.max, ALU.min)
+        def diff_u(job, dst):
+            u[job] = dst
+            diff(dst, n1_t, *job)
 
-        def lower(t, c0, c1):
-            cols = slice(c0 * CH, c1 * CH)
+        def diff_v(job, dst):
+            v[job] = dst
+            diff(dst, n2_t, *job)
+
+        def by_chunk(ap):
+            return ap.rearrange("p (c n) -> p c n", n=CH)
+
+        def raise_v(job, dst):
+            low[job] = dst
+            nc.vector.scalar_tensor_tensor(dst, u[job], 0.0, v[job], ALU.min, ALU.max)
+
+        def turn(bank, src, start, stop):
+            for c in range(NCH):
+                cols = slice(c * CH, (c + 1) * CH)
+                nc.tensor.matmul(
+                    bank[:, cols], src[:, cols], ident[:],
+                    start=start and c == 0, stop=stop and c == NCH - 1, is_transpose=True,
+                )
+
+        def open_sums(job, banks):
+            t = job[0]
+            q = sb.tile([P, S], F32, name="q%d" % t)
+            nc.scalar.activation(q[:], u[job], RELU, scale=-1.0)
+            q_ps = ps.tile([P, S], F32, name="q_ps%d" % t, tag=banks[0])
+            turn(q_ps, q, True, True)
+            sum_ps = ps.tile([P, S], F32, name="sum_ps%d" % t, tag=banks[1])
+            turn(sum_ps, q, True, False)
+            floor = sb.tile([P, S], F32, name="floor%d" % t)
+            nc.scalar.activation(floor[:], q_ps[:], COPY, scale=-1.0)
+            low_ps = ps.tile([P, S], F32, name="low_ps%d" % t, tag=banks[2])
+            low[job] = low_ps[:]
+            turn(low[job], floor, True, False)
+            return sum_ps
+
+        def close_sums(job, sum_ps):
+            t = job[0]
+            turn(sum_ps, v[job], False, True)
+            lift = sb.tile([P, S], F32, name="lift%d" % t)
+            nc.scalar.activation(lift[:], sum_ps[:], RELU)
+            turn(low[job], lift, False, True)
+
+        def finish(job, c0, c1):
+            t, first = job[:2]
+            cols = slice((c0 - first) * CH, (c1 - first) * CH)
             nc.vector.scalar_tensor_tensor(
-                y[:, c0:c1, t, :], u[t][:, cols].rearrange("p (c n) -> p c n", n=CH), 0.0,
-                low[t][:, cols].rearrange("p (c n) -> p c n", n=CH), ALU.min, ALU.max,
+                y[:, c0:c1, t, :], by_chunk(u[job][:, cols]), 0.0, by_chunk(low[job][:, cols]), ALU.max, ALU.min
             )
+
+        def store(t, c0, c1):
             nc.sync.dma_start(out_rows[:, t, c0:c1, :], y[:, c0:c1, t, :])
 
         def weave(eng, c):
-            dst = yb[c][:].rearrange("p (a i) t -> p a t i", i=4)
-            src = y[:, c, :, :].rearrange("p t (a i) -> p a t i", i=4)
+            dst = woven(yb[:, c * CH : (c + 1) * CH, :])
+            src = planes(y[:, c, :, :])
             if eng == "scalar":
                 nc.scalar.copy(dst, src)
             else:
                 nc.vector.tensor_copy(dst, src)
 
-        def quant_y(c):
-            cols = slice(c * CH, (c + 1) * CH)
-            nc.vector.quantize_mx(y_w[:, cols].bitcast(FP8X4), y_s[:, cols], yb[c][:].rearrange("p n t -> p (n t)"))
+        def quant_y(c0, c1):
+            cols = slice(c0 * CH, c1 * CH)
+            nc.vector.quantize_mx(y_w[:, cols].bitcast(FP8X4), y_s[:, cols], yb[:, cols, :].rearrange("p n t -> p (n t)"))
 
-        jobs = [(0, 0, 4), (1, 0, 4), (2, 0, 4), (3, 0, 2), (3, 2, 3), (3, 3, 4)]
-        diff(u, n1_t, 0, 0, 2)
-        diff(u, n1_t, 0, 2, 4)
-        diff(v, n2_t, 0, 0, 4)
-        for i, job in enumerate(jobs):
-            nxt = jobs[i + 1] if i + 1 < len(jobs) else None
-            if nxt:
-                diff(u, n1_t, *nxt)
-            upper(*job)
-            if nxt:
-                diff(v, n2_t, *nxt)
-            else:
-                quant_y(0)
-            lower(*job)
-            if not nxt:
-                quant_y(1)
-                nc.scalar.dma_start(out_words[:, 0 : 2 * CH], y_w[:, 0 : 2 * CH])
-            if job[0] == 3:
-                for c in range(job[1], job[2]):
-                    weave("scalar" if c < NCH - 1 else "vector", c)
-        quant_y(2)
-        quant_y(3)
+        j0, j1, j2, j3a, j3b, j3c = (0, 0, 4), (1, 0, 4), (2, 0, 4), (3, 0, 2), (3, 2, 3), (3, 3, 4)
+        work = [sb.tile([P, S], F32, name="work%d" % i) for i in range(7)]
+        wide = sb.tile([P, 2 * S], F32, name="wide")
+        u[j0] = work[0][:]
+        diff(u[j0][:, : 2 * CH], n1_t, 0, 0, 2)
+        diff(u[j0][:, 2 * CH :], n1_t, 0, 2, 4)
+        sum0 = open_sums(j0, ("bank0", "bank1", "bank2"))
+        diff_v(j0, work[1][:])
+        close_sums(j0, sum0)
+        drain(2)
+        diff_u(j1, wide[:, 2 * CH : 6 * CH])
+        sum1 = open_sums(j1, ("bank3", "bank4", "bank5"))
+        diff_v(j1, work[2][:])
+        drain(3)
+        close_sums(j1, sum1)
+        diff_u(j2, work[3][:])
+        diff_v(j2, work[4][:])
+        diff_u(j3a, work[5][:, : 2 * CH])
+        diff_v(j3a, work[5][:, 2 * CH :])
+        finish(j0, 0, 4)
+        store(0, 0, 4)
+        finish(j1, 0, 2)
+        finish(j1, 2, 4)
+        store(1, 0, 4)
+        raise_v(j2, wide[:, : 4 * CH])
+        raise_v(j3a, wide[:, 4 * CH : 6 * CH])
+        finish(j2, 0, 4)
+        store(2, 0, 4)
+        finish(j3a, 0, 2)
+        store(3, 0, 2)
+        weave("scalar", 0)
+        weave("scalar", 1)
+        diff_u(j3b, work[4][:, 0:CH])
+        diff_v(j3b, work[4][:, CH : 2 * CH])
+        diff_u(j3c, work[4][:, 2 * CH : 3 * CH])
+        diff_v(j3c, work[4][:, 3 * CH :])
+        raise_v(j3b, work[6][:, :CH])
+        raise_v(j3c, work[6][:, CH : 2 * CH])
+        finish(j3b, 2, 3)
+        weave("scalar", 2)
+        finish(j3c, 3, 4)
+        store(3, 2, 4)
+        quant_y(0, 2)
+        nc.scalar.dma_start(out_words[:, 0 : 2 * CH], y_w[:, 0 : 2 * CH])
+        weave("vector", 3)
+        quant_y(2, 3)
+        quant_y(3, 4)
         nc.sync.dma_start(out_words[:, 2 * CH :], y_w[:, 2 * CH :])
         for q in range(4):
             eng = nc.sync if q < 1 else nc.scalar

@@ -23,7 +23,6 @@ PACK = 4
 CH = 128
 NCH = S // CH
 SCORE = 0.0625
-XS_SPLIT = 1344
 
 
 def tile_picked_candmed_none_po_kernel(
@@ -48,16 +47,15 @@ def tile_picked_candmed_none_po_kernel(
         gs_t = sb.tile([P, PACK], F32, name="gs_t")
         zero = sb.tile([P, 1], F32, name="zero")
 
-        nc.vector.memset(xs[:, : XS_SPLIT].bitcast(I32), 0)
-        nc.gpsimd.memset(xs[:, XS_SPLIT :].bitcast(I32), 0)
+        nc.vector.memset(xs[:].bitcast(I32), 0)
         nc.vector.memset(w1s[:].bitcast(I32), 0)
         nc.vector.memset(zero[:], 0.0)
 
         nc.sync.dma_start(w1w[:], w1_words[0].rearrange("p n t -> p (n t)").bitcast(I32))
         nc.sync.dma_start(offs_t[:], offs)
+        nc.sync.dma_start(cand_t[:], cand)
         for q in range(4):
             nc.sync.dma_start(xs[32 * q : 32 * q + 4, :].bitcast(I32), x_scales[0, 4 * q : 4 * q + 4, :].bitcast(I32))
-        nc.sync.dma_start(cand_t[:], cand)
         nc.sync.dma_start(xw[:], x_words[0].rearrange("p n t -> p (n t)").bitcast(I32))
         for q in range(4):
             nc.sync.dma_start(w1s[32 * q : 32 * q + 4, :].bitcast(I32), w1_scales[0, 4 * q : 4 * q + 4, :].bitcast(I32))
@@ -100,7 +98,7 @@ def tile_picked_candmed_none_po_kernel(
             )
 
         hb = [ps.tile([P, PACK, CH], F32, name="hb%d" % c, tag="bank%d" % c) for c in range(NCH)]
-        for c in (2, 0, 1, 3):
+        for c in (2, 3, 0, 1):
             cols = slice(c * CH, (c + 1) * CH)
             for t in range(PACK):
                 m = slice(t * P, (t + 1) * P)
@@ -153,21 +151,25 @@ def tile_picked_candmed_none_po_kernel(
         def drain_pos(bank, t, cols):
             nc.scalar.activation(pos[t][:, cols], bank, COPY, scale=SCORE)
 
-        halves = [slice(0, 2 * CH), slice(2 * CH, S)]
-        gate(0)
-        gate(1)
-        gate(3)
-        first = []
-        for h, cols in enumerate(halves):
-            nc.vector.quantize_mx(z_w[:, cols].bitcast(FP8X4), z_s[:, cols], zb[h][:].rearrange("p n t -> p (n t)"))
-            bank = ps.tile([P, 2 * CH], F32, name="first%d" % h, tag="bank%d" % (4 - h))
+        def first_scores(c0, c1, tag):
+            cols = slice(c0 * CH, c1 * CH)
+            src = zb[c0 // 2][:, c0 % 2 * CH : c0 % 2 * CH + (c1 - c0) * CH, :]
+            nc.vector.quantize_mx(z_w[:, cols].bitcast(FP8X4), z_s[:, cols], src.rearrange("p n t -> p (n t)"))
+            bank = ps.tile([P, (c1 - c0) * CH], F32, name="first%d" % c0, tag=tag)
             score(bank[:], 0, xc_s0[:], cols)
             drain_neg(bank[:], 0, cols)
-            first.append(bank)
-        drain_pos(first[1][:], 0, halves[1])
-        xc_s = sb.tile([P, (PACK - 1) * P], U8, name="xc_s", tag="zb1", align_bytes=64)
+            return bank, cols
+
+        gate(3)
+        gate(0)
+        bank, cols = first_scores(2, 4, "bank4")
+        drain_pos(bank[:], 0, cols)
+        gate(1)
+        late = [first_scores(0, 1, "bank0"), first_scores(1, 2, "bank1")]
+        for bank, cols in late:
+            drain_pos(bank[:], 0, cols)
+        xc_s = sb.tile([P, (PACK - 1) * P], U8, name="xc_s", tag="zb0", align_bytes=64)
         nc.vector.tensor_copy(xc_s[:].rearrange("p (t m) -> p m t", t=PACK - 1), xc_mt[:, :, 1:])
-        nc.vector.tensor_scalar_mul(pos[0][:, halves[0]], first[0][:], SCORE)
         score_ps = {}
         for t in range(1, PACK):
             score_ps[t] = ps.tile([P, S], F32, name="sb%d" % t, tag="bank%d" % (NCH + t))
@@ -260,16 +262,16 @@ def tile_picked_candmed_none_po_kernel(
 
         j0, j1, j2, j3a, j3b, j3c = (0, 0, 4), (1, 0, 4), (2, 0, 4), (3, 0, 2), (3, 2, 3), (3, 3, 4)
         work = [sb.tile([P, S], F32, name="work%d" % i) for i in range(7)]
-        wide = sb.tile([P, 2 * S], F32, name="wide")
-        u[j0] = work[0][:]
-        diff(u[j0][:, : 2 * CH], n1_t, 0, 0, 2)
+        wide = sb.tile([P, 6 * CH], F32, name="wide")
+        u[j0] = wide[:, 2 * CH :]
         diff(u[j0][:, 2 * CH :], n1_t, 0, 2, 4)
-        sum0 = open_sums(j0, ("bank0", "bank1", "bank2"))
+        diff(u[j0][:, : 2 * CH], n1_t, 0, 0, 2)
+        sum0 = open_sums(j0, ("bank2", "bank3", "bank4"))
         diff_v(j0, work[1][:])
         close_sums(j0, sum0)
         drain(2)
-        diff_u(j1, wide[:, 2 * CH : 6 * CH])
-        sum1 = open_sums(j1, ("bank3", "bank4", "bank5"))
+        diff_u(j1, work[0][:])
+        sum1 = open_sums(j1, ("bank0", "bank1", "bank5"))
         diff_v(j1, work[2][:])
         drain(3)
         close_sums(j1, sum1)
@@ -277,23 +279,24 @@ def tile_picked_candmed_none_po_kernel(
         diff_v(j2, work[4][:])
         diff_u(j3a, work[5][:, : 2 * CH])
         diff_v(j3a, work[5][:, 2 * CH :])
-        finish(j0, 0, 4)
+        finish(j0, 0, 2)
+        finish(j0, 2, 4)
         store(0, 0, 4)
-        finish(j1, 0, 2)
-        finish(j1, 2, 4)
-        store(1, 0, 4)
         raise_v(j2, wide[:, : 4 * CH])
-        raise_v(j3a, wide[:, 4 * CH : 6 * CH])
+        raise_v(j3a, wide[:, 4 * CH :])
         finish(j2, 0, 4)
         store(2, 0, 4)
         finish(j3a, 0, 2)
         store(3, 0, 2)
+        finish(j1, 0, 2)
         weave("scalar", 0)
         weave("scalar", 1)
-        diff_u(j3b, work[4][:, 0:CH])
-        diff_v(j3b, work[4][:, CH : 2 * CH])
-        diff_u(j3c, work[4][:, 2 * CH : 3 * CH])
-        diff_v(j3c, work[4][:, 3 * CH :])
+        finish(j1, 2, 4)
+        store(1, 0, 4)
+        diff_u(j3b, work[0][:, 0:CH])
+        diff_v(j3b, work[0][:, CH : 2 * CH])
+        diff_u(j3c, work[0][:, 2 * CH : 3 * CH])
+        diff_v(j3c, work[0][:, 3 * CH :])
         raise_v(j3b, work[6][:, :CH])
         raise_v(j3c, work[6][:, CH : 2 * CH])
         finish(j3b, 2, 3)

@@ -66,10 +66,9 @@ def tile_picked_candmed_none_po_kernel(
         ident = sb.tile([P, P], F32, name="ident")
         make_identity(nc, ident[:])
 
-        win = [sb.tile([P, 2 * S if t < 3 else S], F32, name="win%d" % t) for t in range(PACK)]
-        s2 = sb.tile([P, S], F32, name="s2")
+        win = [sb.tile([P, 2 * S], F32, name="win%d" % t) for t in range(PACK)]
         s3 = sb.tile([P, S], F32, name="s3")
-        pos = [win[1][:, S:], win[2][:, S:], s2[:], s3[:]]
+        pos = [win[1][:, S:], win[2][:, S:], win[3][:, S:], s3[:]]
         nc.scalar.activation(win[0][:, S:], zero[:].to_broadcast([P, S]), COPY)
 
         xq_w = [
@@ -216,10 +215,13 @@ def tile_picked_candmed_none_po_kernel(
                     start=start and c == 0, stop=stop and c == NCH - 1, is_transpose=True,
                 )
 
-        def open_sums(job, banks):
-            t = job[0]
-            q = sb.tile([P, S], F32, name="q%d" % t)
+        def below_zero(job):
+            q = sb.tile([P, S], F32, name="q%d" % job[0])
             nc.scalar.activation(q[:], u[job], RELU, scale=-1.0)
+            return q
+
+        def open_sums(job, q, banks):
+            t = job[0]
             q_ps = ps.tile([P, S], F32, name="q_ps%d" % t, tag=banks[0])
             turn(q_ps, q, True, True)
             sum_ps = ps.tile([P, S], F32, name="sum_ps%d" % t, tag=banks[1])
@@ -231,10 +233,8 @@ def tile_picked_candmed_none_po_kernel(
             turn(low[job], floor, True, False)
             return sum_ps
 
-        def close_sums(job, sum_ps):
-            t = job[0]
-            turn(sum_ps, v[job], False, True)
-            lift = sb.tile([P, S], F32, name="lift%d" % t)
+        def close_low(job, sum_ps):
+            lift = sb.tile([P, S], F32, name="lift%d" % job[0])
             nc.scalar.activation(lift[:], sum_ps[:], RELU)
             turn(low[job], lift, False, True)
 
@@ -266,19 +266,26 @@ def tile_picked_candmed_none_po_kernel(
         u[j0] = wide[:, 2 * CH :]
         diff(u[j0][:, 2 * CH :], n1_t, 0, 2, 4)
         diff(u[j0][:, : 2 * CH], n1_t, 0, 0, 2)
-        sum0 = open_sums(j0, ("bank2", "bank3", "bank4"))
-        diff_v(j0, work[1][:])
-        close_sums(j0, sum0)
+        q0 = below_zero(j0)
         drain(2)
+        sum0 = open_sums(j0, q0, ("bank2", "bank3", "bank4"))
+        diff_v(j0, work[1][:])
+        turn(sum0, v[j0], False, True)
         diff_u(j1, work[0][:])
-        sum1 = open_sums(j1, ("bank0", "bank1", "bank5"))
-        diff_v(j1, work[2][:])
+        q1 = below_zero(j1)
         drain(3)
-        close_sums(j1, sum1)
+        close_low(j0, sum0)
+        sum1 = open_sums(j1, q1, ("bank0", "bank1", "bank5"))
+        diff_v(j1, work[2][:])
+        turn(sum1, v[j1], False, True)
+        close_low(j1, sum1)
         diff_u(j2, work[3][:])
         diff_v(j2, work[4][:])
-        diff_u(j3a, work[5][:, : 2 * CH])
-        diff_v(j3a, work[5][:, 2 * CH :])
+        diff(work[5][:], n1_t, 3, 0, 4)
+        diff(work[6][:], n2_t, 3, 0, 4)
+        for job in (j3a, j3b, j3c):
+            u[job] = work[5][:, job[1] * CH : job[2] * CH]
+            v[job] = work[6][:, job[1] * CH : job[2] * CH]
         finish(j0, 0, 2)
         finish(j0, 2, 4)
         store(0, 0, 4)
@@ -293,21 +300,17 @@ def tile_picked_candmed_none_po_kernel(
         weave("scalar", 1)
         finish(j1, 2, 4)
         store(1, 0, 4)
-        diff_u(j3b, work[0][:, 0:CH])
-        diff_v(j3b, work[0][:, CH : 2 * CH])
-        diff_u(j3c, work[0][:, 2 * CH : 3 * CH])
-        diff_v(j3c, work[0][:, 3 * CH :])
-        raise_v(j3b, work[6][:, :CH])
-        raise_v(j3c, work[6][:, CH : 2 * CH])
+        raise_v(j3b, work[0][:, :CH])
+        raise_v(j3c, work[0][:, 2 * CH : 3 * CH])
         finish(j3b, 2, 3)
         weave("scalar", 2)
         finish(j3c, 3, 4)
         store(3, 2, 4)
+        weave("vector", 3)
         quant_y(0, 2)
         nc.scalar.dma_start(out_words[:, 0 : 2 * CH], y_w[:, 0 : 2 * CH])
-        weave("vector", 3)
-        quant_y(2, 3)
         quant_y(3, 4)
+        quant_y(2, 3)
         nc.sync.dma_start(out_words[:, 2 * CH :], y_w[:, 2 * CH :])
         for q in range(4):
             eng = nc.sync if q < 1 else nc.scalar

from contextlib import ExitStack

import concourse.mybir as mybir
from concourse.masks import make_identity

K, T, S, H, C = 512, 2048, 512, 512, 512
FLOPS = 2 * K * H * S + 2 * K * C * S
BYTES = K * (S + C) * 33 // 32 + K * H * 33 // 32 + 4 * K + 4 * 128 * 32 * 2 + C * S * 4 + C * S * 33 // 32

F32 = mybir.dt.float32
BF16 = mybir.dt.bfloat16
I32 = mybir.dt.int32
U32 = mybir.dt.uint32
U16 = mybir.dt.uint16
U8 = mybir.dt.uint8
FP8X4 = mybir.dt.float8_e4m3fn_x4
ALU = mybir.AluOpType
COPY = mybir.ActivationFunctionType.Copy
RELU = mybir.ActivationFunctionType.Relu

P = 128
PACK = 4
CH = 128
NCH = S // CH
SCORE = 0.0625


def tile_picked_candmed_none_po_kernel(
    tc, x_words, x_scales, w1_words, w1_scales, gs, offs, cand, n1, n2, out_0, out_1, out_2
):
    nc = tc.nc
    with ExitStack() as ctx:
        lists = ctx.enter_context(tc.tile_pool(name="lists", bufs=1))
        sb = ctx.enter_context(tc.tile_pool(name="sb", bufs=1))
        reuse = ctx.enter_context(tc.tile_pool(name="reuse", bufs=1))
        ps = ctx.enter_context(tc.psum_pool(name="ps", bufs=1))

        offs_t = lists.tile([P, S // 16], U16, name="offs_t")
        cand_t = lists.tile([P, C // 16], U16, name="cand_t")
        n1_t = lists.tile([P, S // 16], U16, name="n1_t")
        n2_t = lists.tile([P, S // 16], U16, name="n2_t")

        xw = sb.tile([P, T], I32, name="xw", align_bytes=64)
        xs = sb.tile([P, T], U8, name="xs", align_bytes=64)
        w1w = sb.tile([P, H], I32, name="w1w", align_bytes=64)
        w1s = reuse.tile([P, H], U8, name="w1s", offset=768, align_bytes=64)
        gs_t = sb.tile([P, PACK], F32, name="gs_t")
        zero = sb.tile([P, 1], F32, name="zero")

        nc.vector.memset(xs[:].bitcast(I32), 0)
        nc.vector.memset(w1s[:].bitcast(I32), 0)
        nc.vector.memset(zero[:], 0.0)

        nc.sync.dma_start(w1w[:], w1_words[0].rearrange("p n t -> p (n t)").bitcast(I32))
        nc.sync.dma_start(offs_t[:], offs)
        nc.sync.dma_start(cand_t[:], cand)
        for q in range(4):
            nc.sync.dma_start(xs[32 * q : 32 * q + 4, :].bitcast(I32), x_scales[0, 4 * q : 4 * q + 4, :].bitcast(I32))
        nc.sync.dma_start(xw[:], x_words[0].rearrange("p n t -> p (n t)").bitcast(I32))
        for q in range(4):
            nc.sync.dma_start(w1s[32 * q : 32 * q + 4, :].bitcast(I32), w1_scales[0, 4 * q : 4 * q + 4, :].bitcast(I32))
        nc.sync.dma_start(gs_t[:], gs.rearrange("(p t) o -> p (t o)", t=PACK))
        nc.sync.dma_start(n1_t[:], n1)
        nc.sync.dma_start(n2_t[:], n2)

        ident = sb.tile([P, P], F32, name="ident")
        make_identity(nc, ident[:])

        win = [sb.tile([P, 2 * S], F32, name="win%d" % t) for t in range(PACK)]
        s3 = sb.tile([P, S], F32, name="s3")
        pos = [win[1][:, S:], win[2][:, S:], win[3][:, S:], s3[:]]
        nc.scalar.activation(win[0][:, S:], zero[:].to_broadcast([P, S]), COPY)

        xq_w = [
            reuse.tile([P, S // 2], I32, name="xq_w0", offset=0, align_bytes=64),
            sb.tile([P, S // 2], I32, name="xq_w1", align_bytes=64),
        ]
        xq_s = sb.tile([P, S], U8, name="xq_s", align_bytes=64)
        xc_raw = sb.tile([P, C], U8, name="xc_raw", align_bytes=64)
        xc_s0 = sb.tile([P, P], U8, name="xc_s0", align_bytes=64)
        wd_w = sb.tile([P, H], I32, name="wd_w", align_bytes=64)
        wd_s = sb.tile([P, H], U8, name="wd_s", align_bytes=64)

        def deal(dst, src):
            nc.vector.tensor_copy(dst.rearrange("p (t m) -> p m t", t=PACK), src.rearrange("p (m t) -> p m t", t=PACK))

        deal(wd_w[:], w1w[:])
        nc.vector.tensor_copy(xq_s[:], xs[:].indirect(offs_t[:]))
        nc.vector.tensor_copy(xc_raw[:], xs[:].indirect(cand_t[:]))
        xc_mt = xc_raw[:].rearrange("p (m t) -> p m t", t=PACK)
        nc.vector.tensor_copy(xc_s0[:], xc_mt[:, :, 0])
        deal(wd_s[:], w1s[:])
        for half in (1, 0):
            nc.vector.tensor_copy(
                xq_w[half][:].bitcast(U32),
                xw[:].bitcast(U32).indirect(offs_t[:, 16 * half : 16 * (half + 1)]),
            )

        hb = [ps.tile([P, PACK, CH], F32, name="hb%d" % c, tag="bank%d" % c) for c in range(NCH)]
        for c in (2, 3, 0, 1):
            cols = slice(c * CH, (c + 1) * CH)
            for t in range(PACK):
                m = slice(t * P, (t + 1) * P)
                nc.tensor.matmul_mx(
                    hb[c][:, t, :], lhsT=wd_w[:, m].bitcast(FP8X4), lhsT_scale=wd_s[:, m],
                    rhs=xq_w[c // 2][:, c % 2 * CH : (c % 2 + 1) * CH].bitcast(FP8X4), rhs_scale=xq_s[:, cols], start=True, stop=True,
                )

        xc_w = reuse.tile([P, C], I32, name="xc_w", offset=1024, align_bytes=64)
        nc.vector.tensor_copy(
            xc_w[:].bitcast(U32).rearrange("p (t m) -> p m t", t=PACK), xw[:].bitcast(U32).indirect(cand_t[:])
        )

        zb = [sb.tile([P, 2 * CH, PACK], BF16, name="zb%d" % h, tag="zb%d" % h, align_bytes=64) for h in range(2)]

        def z_chunk(c):
            return zb[c // 2][:, c % 2 * CH : (c % 2 + 1) * CH, :]

        z_w = sb.tile([P, S], I32, name="z_w", align_bytes=64)
        z_s = sb.tile([P, S], U8, name="z_s", align_bytes=64)

        def woven(tile3):
            return tile3.rearrange("p (a i) t -> p a t i", i=4)

        def planes(tile3):
            return tile3.rearrange("p t (a i) -> p a t i", i=4)

        h0 = sb.tile([P, PACK, CH], F32, name="h0")
        z0 = sb.tile([P, PACK, CH], BF16, name="z0")
        nc.scalar.activation(h0[:], hb[2][:], RELU)
        for t in range(PACK):
            nc.scalar.activation(z0[:, t, :], h0[:, t, :], COPY, scale=gs_t[:, t : t + 1])
        nc.scalar.copy(woven(z_chunk(2)), planes(z0[:]))

        def gate(c):
            nc.vector.scalar_tensor_tensor(
                z_chunk(c), hb[c][:].rearrange("p t n -> p n t"), 0.0,
                gs_t[:].unsqueeze(1).to_broadcast([P, CH, PACK]), ALU.max, ALU.mult,
            )

        def score(bank, t, scales, cols):
            nc.tensor.matmul_mx(
                bank, lhsT=xc_w[:, t * P : (t + 1) * P].bitcast(FP8X4), lhsT_scale=scales,
                rhs=z_w[:, cols].bitcast(FP8X4), rhs_scale=z_s[:, cols], start=True, stop=True,
            )

        def drain_neg(bank, t, cols):
            nc.scalar.activation(win[t][:, cols], bank, COPY, scale=-SCORE)

        def drain_pos(bank, t, cols):
            nc.scalar.activation(pos[t][:, cols], bank, COPY, scale=SCORE)

        def first_scores(c0, c1, tag):
            cols = slice(c0 * CH, c1 * CH)
            src = zb[c0 // 2][:, c0 % 2 * CH : c0 % 2 * CH + (c1 - c0) * CH, :]
            nc.vector.quantize_mx(z_w[:, cols].bitcast(FP8X4), z_s[:, cols], src.rearrange("p n t -> p (n t)"))
            bank = ps.tile([P, (c1 - c0) * CH], F32, name="first%d" % c0, tag=tag)
            score(bank[:], 0, xc_s0[:], cols)
            drain_neg(bank[:], 0, cols)
            return bank, cols

        gate(3)
        gate(0)
        bank, cols = first_scores(2, 4, "bank4")
        drain_pos(bank[:], 0, cols)
        gate(1)
        late = [first_scores(0, 1, "bank0"), first_scores(1, 2, "bank1")]
        for bank, cols in late:
            drain_pos(bank[:], 0, cols)
        xc_s = sb.tile([P, (PACK - 1) * P], U8, name="xc_s", tag="zb0", align_bytes=64)
        nc.vector.tensor_copy(xc_s[:].rearrange("p (t m) -> p m t", t=PACK - 1), xc_mt[:, :, 1:])
        score_ps = {}
        for t in range(1, PACK):
            score_ps[t] = ps.tile([P, S], F32, name="sb%d" % t, tag="bank%d" % (NCH + t))
            score(score_ps[t][:], t, xc_s[:, (t - 1) * P : t * P], slice(0, S))

        def drain(t):
            drain_neg(score_ps[t][:], t, slice(0, S))
            drain_pos(score_ps[t][:], t, slice(0, S))

        drain(1)

        u, v, low = {}, {}, {}
        y = sb.tile([P, NCH, PACK, CH], F32, name="y", align_bytes=64)
        yb = sb.tile([P, S, PACK], BF16, name="yb", align_bytes=64)
        y_w = sb.tile([P, S], I32, name="y_w", align_bytes=64)
        y_s = sb.tile([P, S], U8, name="y_s", align_bytes=64)
        out_rows = out_0.rearrange("(p t) (c n) -> p t c n", t=PACK, n=CH)
        out_words = out_1[0].rearrange("p n t -> p (n t)").bitcast(I32)

        def diff(dst, lst, t, c0, c1):
            cols = slice(c0 * CH, c1 * CH)
            nc.vector.tensor_tensor(dst, win[t][:].indirect(lst[:, c0 * CH // 16 : c1 * CH // 16]), pos[t][:, cols], ALU.add)

        def diff_u(job, dst):
            u[job] = dst
            diff(dst, n1_t, *job)

        def diff_v(job, dst):
            v[job] = dst
            diff(dst, n2_t, *job)

        def by_chunk(ap):
            return ap.rearrange("p (c n) -> p c n", n=CH)

        def raise_v(job, dst):
            low[job] = dst
            nc.vector.scalar_tensor_tensor(dst, u[job], 0.0, v[job], ALU.min, ALU.max)

        def turn(bank, src, start, stop):
            for c in range(NCH):
                cols = slice(c * CH, (c + 1) * CH)
                nc.tensor.matmul(
                    bank[:, cols], src[:, cols], ident[:],
                    start=start and c == 0, stop=stop and c == NCH - 1, is_transpose=True,
                )

        def below_zero(job):
            q = sb.tile([P, S], F32, name="q%d" % job[0])
            nc.scalar.activation(q[:], u[job], RELU, scale=-1.0)
            return q

        def open_sums(job, q, banks):
            t = job[0]
            q_ps = ps.tile([P, S], F32, name="q_ps%d" % t, tag=banks[0])
            turn(q_ps, q, True, True)
            sum_ps = ps.tile([P, S], F32, name="sum_ps%d" % t, tag=banks[1])
            turn(sum_ps, q, True, False)
            floor = sb.tile([P, S], F32, name="floor%d" % t)
            nc.scalar.activation(floor[:], q_ps[:], COPY, scale=-1.0)
            low_ps = ps.tile([P, S], F32, name="low_ps%d" % t, tag=banks[2])
            low[job] = low_ps[:]
            turn(low[job], floor, True, False)
            return sum_ps

        def close_low(job, sum_ps):
            lift = sb.tile([P, S], F32, name="lift%d" % job[0])
            nc.scalar.activation(lift[:], sum_ps[:], RELU)
            turn(low[job], lift, False, True)

        def finish(job, c0, c1):
            t, first = job[:2]
            cols = slice((c0 - first) * CH, (c1 - first) * CH)
            nc.vector.scalar_tensor_tensor(
                y[:, c0:c1, t, :], by_chunk(u[job][:, cols]), 0.0, by_chunk(low[job][:, cols]), ALU.max, ALU.min
            )

        def store(t, c0, c1):
            nc.sync.dma_start(out_rows[:, t, c0:c1, :], y[:, c0:c1, t, :])

        def weave(eng, c):
            dst = woven(yb[:, c * CH : (c + 1) * CH, :])
            src = planes(y[:, c, :, :])
            if eng == "scalar":
                nc.scalar.copy(dst, src)
            else:
                nc.vector.tensor_copy(dst, src)

        def quant_y(c0, c1):
            cols = slice(c0 * CH, c1 * CH)
            nc.vector.quantize_mx(y_w[:, cols].bitcast(FP8X4), y_s[:, cols], yb[:, cols, :].rearrange("p n t -> p (n t)"))

        j0, j1, j2, j3a, j3b, j3c = (0, 0, 4), (1, 0, 4), (2, 0, 4), (3, 0, 2), (3, 2, 3), (3, 3, 4)
        work = [sb.tile([P, S], F32, name="work%d" % i) for i in range(7)]
        wide = sb.tile([P, 6 * CH], F32, name="wide")
        u[j0] = wide[:, 2 * CH :]
        diff(u[j0][:, 2 * CH :], n1_t, 0, 2, 4)
        diff(u[j0][:, : 2 * CH], n1_t, 0, 0, 2)
        q0 = below_zero(j0)
        drain(2)
        sum0 = open_sums(j0, q0, ("bank2", "bank3", "bank4"))
        diff_v(j0, work[1][:])
        turn(sum0, v[j0], False, True)
        diff_u(j1, work[0][:])
        q1 = below_zero(j1)
        drain(3)
        close_low(j0, sum0)
        sum1 = open_sums(j1, q1, ("bank0", "bank1", "bank5"))
        diff_v(j1, work[2][:])
        turn(sum1, v[j1], False, True)
        close_low(j1, sum1)
        diff_u(j2, work[3][:])
        diff_v(j2, work[4][:])
        diff(work[5][:], n1_t, 3, 0, 4)
        diff(work[6][:], n2_t, 3, 0, 4)
        for job in (j3a, j3b, j3c):
            u[job] = work[5][:, job[1] * CH : job[2] * CH]
            v[job] = work[6][:, job[1] * CH : job[2] * CH]
        finish(j0, 0, 2)
        finish(j0, 2, 4)
        store(0, 0, 4)
        raise_v(j2, wide[:, : 4 * CH])
        raise_v(j3a, wide[:, 4 * CH :])
        finish(j2, 0, 4)
        store(2, 0, 4)
        finish(j3a, 0, 2)
        store(3, 0, 2)
        finish(j1, 0, 2)
        weave("scalar", 0)
        weave("scalar", 1)
        finish(j1, 2, 4)
        store(1, 0, 4)
        raise_v(j3b, work[0][:, :CH])
        raise_v(j3c, work[0][:, 2 * CH : 3 * CH])
        finish(j3b, 2, 3)
        weave("scalar", 2)
        finish(j3c, 3, 4)
        store(3, 2, 4)
        weave("vector", 3)
        quant_y(0, 2)
        nc.scalar.dma_start(out_words[:, 0 : 2 * CH], y_w[:, 0 : 2 * CH])
        quant_y(3, 4)
        quant_y(2, 3)
        nc.sync.dma_start(out_words[:, 2 * CH :], y_w[:, 2 * CH :])
        for q in range(4):
            eng = nc.sync if q < 1 else nc.scalar
            eng.dma_start(out_2[0, 4 * q : 4 * q + 4, :].bitcast(I32), y_s[32 * q : 32 * q + 4, :].bitcast(I32))
